import numpy as np, ml_dtypes
CORES = [23,119,17,113]
N = 4
BF = ml_dtypes.bfloat16
def gentries(a):
    return np.ascontiguousarray(a.reshape(8, 16, -1).transpose(0, 2, 1)).reshape(8, -1)
def gtable(e):
    e = np.asarray(e); return np.ascontiguousarray(e.reshape(8, -1, 16).transpose(0, 2, 1)).reshape(128, -1).astype(np.int32)
def f(rng, *shape):
    return (rng.standard_normal(shape, dtype=np.float32) * np.exp2(rng.integers(-2, 3, shape[:-1] + (1,)))).astype(BF)
def wide(rng, *shape):
    v = f(rng, *shape).astype(np.float32); k = shape[:-2] + (1, shape[-1])
    return (v * np.exp2(rng.integers(-6, 7, k)) * (rng.random(k) > 0.0625)).astype(BF)
LV, M, S = 5, 768, 48
R, A = LV * M, (LV - 1) * (N - 1) * S
W, K = R + A, 4 * M * (LV - 1)
LEV4 = np.repeat(np.concatenate([np.arange(R) // M, np.arange(A) // ((N - 1) * S)]), 4)
OWN4 = np.repeat(np.arange(W) < R, 4).astype(np.float64)
def draw_ent(rng, pri, tidy):
    e = np.zeros((8, LV - 1, 4, M), np.int64)
    for g in range(8):
        free = np.ones(4 * W, bool)
        for l in range(1, LV):
            c = np.flatnonzero(free & (LEV4 < l)); c = c[np.argsort(pri[c] + rng.random(len(c)))[:4 * M]]; free[c] = False
            e[g, l - 1] = np.sort(c).reshape(M, 4)[rng.permutation(M)].T if tidy else rng.permutation(c).reshape(4, M)
    return gtable(e.reshape(8, -1))
def draw_sl(rng, same):
    s = np.zeros((8, LV - 1, N - 1, S), np.int64)
    for g in range(8):
        for l in range(LV - 1):
            if same:
                u = np.concatenate([[0, M - 1], 1 + rng.permutation(M - 2)[:S - 2]]); v = [rng.permutation(u) for d in range(N - 1)]
            else:
                v = [rng.permutation(M)[:S] for d in range(N - 1)]
            s[g, l] = l * M + np.stack(v)
    return gtable(s.reshape(8, -1))
def draw(rng, pri, tidy, same):
    return {"b": f(rng, N, 128, R), "val": ((rng.random((N, 8, K)) - 0.5) * 0.5).astype(BF),
            "ent": np.stack([draw_ent(rng, pri[r], tidy[r]) for r in range(N)]), "sl": np.stack([draw_sl(rng, same) for r in range(N)])}
def setup_inputs(rng):
    return draw(rng, [0 * OWN4] * N, [False] * N, False)
def setup_inputs_same(rng):
    return draw(rng, [OWN4] * N, [False] * N, True)
def setup_inputs_old(rng):
    return draw(rng, [LEV4.astype(np.float64)] * N, [False] * N, False)
def setup_inputs_mixed(rng):
    o = int(rng.integers(0, 2))
    return draw(rng, [1 - OWN4 if (r + o) % 2 else OWN4 for r in range(N)], [(r + o) % 2 == 1 for r in range(N)], False)
def setup_inputs_strong(rng):
    d = setup_inputs(rng); d["val"] = np.where(rng.random((N, 8, K)) < 0.9, -0.25, 0.25).astype(BF); return d
def setup_inputs_spread(rng):
    d = setup_inputs(rng); d["b"] = wide(rng, N, 128, R)
    d["val"] = (d["val"].astype(np.float32) * np.exp2(-rng.integers(0, 7, (N, 8, K))) * (rng.random((N, 8, K)) > 0.0625)).astype(BF); return d
def check_inputs(d):
    bad = []
    if not np.isfinite(d["b"].astype(np.float32)).all(): bad.append("b finite")
    if not (np.abs(d["val"].astype(np.float32)) <= 0.25).all(): bad.append("size of val")
    lv = np.arange(LV - 1)
    for r in range(N):
        e = gentries(d["ent"][r]).astype(np.int64); s = gentries(d["sl"][r]).astype(np.int64).reshape(8, LV - 1, N - 1, S)
        if (e < 0).any() or (e >= 4 * W).any(): bad.append("ent range")
        elif (LEV4[e].reshape(8, LV - 1, 4 * M) > lv[:, None]).any(): bad.append("ent level")
        if (np.diff(np.sort(e, axis=1), axis=1) == 0).any(): bad.append("ent differ")
        if (s // M != lv[:, None, None]).any(): bad.append("sl level")
        if (np.diff(np.sort(s, axis=3), axis=3) == 0).any(): bad.append("sl differ")
    return sorted(set(bad))
def reference(b, val, ent, sl):
    en = np.stack([gentries(ent[r]) for r in range(N)]).astype(np.int64).reshape(N, 8, LV - 1, 4, M); place = en // 4
    se = np.stack([gentries(sl[r]) for r in range(N)]).astype(np.int64).reshape(N, 8, LV - 1, N - 1, S)
    v = val.astype(np.float64).reshape(N, 8, LV - 1, 4, M)
    w = np.zeros((N, 8, 16, W), np.float64); w[..., :R] = b.astype(np.float64).reshape(N, 8, 16, R)
    for l in range(LV):
        for r in range(N):
            for g in range(8):
                if l > 0: w[r, g, :, l * M:(l + 1) * M] -= np.sum(v[r, g, l - 1] * w[r, g][:, place[r, g, l - 1]], axis=1)
                if l < LV - 1:
                    for d in range(N - 1):
                        m = R + (l * (N - 1) + d) * S
                        w[(r + 1 + d) % N, g, :, m:m + S] = w[r, g][:, se[r, g, l, d]]
    z = np.zeros((N, 8, 16, R), np.float64); bk = np.zeros((N, 8, 16, 4 * W), np.float64)
    for l in range(LV - 1, -1, -1):
        for r in range(N):
            for g in range(8):
                x = w[r, g, :, l * M:(l + 1) * M] - np.sum(bk[r, g, :, 4 * l * M:4 * (l + 1) * M].reshape(16, M, 4), axis=2)
                if l < LV - 1:
                    for d in range(N - 1):
                        m = R + (l * (N - 1) + d) * S
                        x[:, se[r, g, l, d] - l * M] -= np.sum(bk[(r + 1 + d) % N, g, :, 4 * m:4 * (m + S)].reshape(16, S, 4), axis=2)
                z[r, g, :, l * M:(l + 1) * M] = x
                if l > 0: bk[r, g][:, en[r, g, l - 1]] = v[r, g, l - 1] * x[:, None, :]
    return {"z": z.reshape(N, 128, R).astype(np.float32)}

@@ -1,0 +1,310 @@
+from concourse.bass import DstId, RemoteDMATransfer
+from concourse.mybir import AluOpType, ActivationFunctionType
+
+LV, M, S, N = 5, 768, 48, 4
+R, SH = LV * M, (N - 1) * S
+K = 4 * M
+RS = 4 * R
+
+SCRATCH = {
+    "w": ("sbuf", [128, R + 4 * SH], "float32"),
+    "bk": ("sbuf", [128, 4 * (R + 4 * SH)], "float32"),
+    "valf": ("sbuf", [128, 4 * K], "float32"),
+    "bsb": ("sbuf", [128, R], "bfloat16"),
+    "vsb": ("sbuf", [128, 4 * K], "bfloat16"),
+    "ents": ("sbuf", [128, 768], "int32"),
+    "entp": ("sbuf", [128, 768], "int32"),
+    "offf": ("sbuf", [128, 768], "uint16"),
+    "offb": ("sbuf", [128, 768], "uint16"),
+    "slr": ("sbuf", [128, 36], "int32"),
+    "sla": ("sbuf", [128, 40], "uint16"),
+    "slb": ("sbuf", [128, 40], "uint16"),
+    "p0": ("sbuf", [128, M], "float32"),
+    "p1": ("sbuf", [128, M], "float32"),
+    "raw": ("sbuf", [128, 2 * M], "float32"),
+    "t1": ("sbuf", [128, M], "float32"),
+    "t2": ("sbuf", [128, M], "float32"),
+    "sh": ("sbuf", [128, 4 * SH], "float32"),
+    "rsum": ("sbuf", [128, 4 * SH], "float32"),
+    "rc": ("sbuf", [128, 4 * SH], "float32"),
+    "u1": ("sbuf", [128, 2 * SH], "float32"),
+    "tmp": ("sbuf", [128, S], "float32"),
+    "negb": ("sbuf", [128, 128], "bfloat16"),
+    "sel0": ("sbuf", [128, 128], "bfloat16"),
+    "sel": ("sbuf", [128, 128], "bfloat16"),
+    "oneb": ("sbuf", [128, 128], "bfloat16"),
+    "idb": ("sbuf", [128, 128], "bfloat16"),
+    "onef": ("sbuf", [128, 128], "float32"),
+    "idf": ("sbuf", [128, 128], "float32"),
+    "acc": ("psum", [128, 1024], "float32"),
+    "fac": ("psum", [128, 1536], "float32"),
+    "stg": ("psum", [128, 1536], "float32"),
+}
+SEMAPHORES = (["vs", "ss", "ts", "gs", "loc", "st", "ldsl"]
+              + ["ldb%d" % l for l in range(5)] + ["lde%d" % l for l in range(1, 5)]
+              + ["ldv%d" % l for l in range(1, 5)] + ["fa%d" % h for h in range(4)]
+              + ["ba%d_%d" % (h, d) for h in range(4) for d in range(3)])
+
+
+def engine_plan(src, dsts, topo):
+    left = sorted(dsts, key=lambda c: len(topo.engines(src, c)))
+    used, plan = set(), {}
+    for i, c in enumerate(left):
+        free = [e for e in topo.engines(src, c) if e not in used]
+        share = sum(1 for x in left[i:] if set(topo.engines(src, x)) == set(topo.engines(src, c)))
+        n = 1
+        while 2 * n <= len(free) // share and 2 * n <= 4:
+            n *= 2
+        plan[c] = free[:n]
+        used.update(plan[c])
+    return plan
+
+
+def rank_program(g, core, T, topo):
+    rank = T.rank_of(core)
+    if rank is None:
+        return
+    ADD, MUL = AluOpType.add, AluOpType.mult
+    COPY = ActivationFunctionType.Copy
+    cores = list(T.cores)
+    q = {"v": g.vector, "s": g.scalar, "t": g.tensor, "g": g, "y": g.sync}
+    own = {"v": "vs", "s": "ss", "t": "ts", "g": "gs"}
+    count = {"vs": 0, "ss": 0, "ts": 0, "gs": 0}
+    seen = {k: {} for k in q}
+
+    def wait(k, *tokens):
+        need = {}
+        for name, n in tokens:
+            if n > need.get(name, 0):
+                need[name] = n
+        for name, n in need.items():
+            if n > seen[k].get(name, 0):
+                q[k].wait_ge(T.sem[name], n)
+                seen[k][name] = n
+
+    def done(k, ins):
+        name = own[k]
+        ins.then_inc(T.sem[name], 1)
+        count[name] += 1
+        return (name, count[name])
+
+    others = [c for c in cores if c != core]
+    plan = engine_plan(core, others, topo)
+    arrive = {c: len(engine_plan(c, [x for x in cores if x != c], topo)[core]) for c in others}
+
+    def send(h, src, dst, dst_base, forward):
+        tr = []
+        for d in range(3):
+            c = cores[(rank + 1 + d) % N] if forward else cores[(rank - 1 - d) % N]
+            rid, pid = topo.addr(c)[:2]
+            a = (h * 3 + d) * S
+            m = sum(1 << e for e in plan[c])
+            sem = T.sem["fa%d" % h] if forward else T.sem["ba%d_%d" % (h, d)]
+            tr.append(RemoteDMATransfer(dst_ids=[DstId(rid=rid, pnc=pid)], dma_engine_mask=m, remote_sem=sem,
+                                        srcs=[src[:, a:a + S]], dsts=[dst[:, dst_base + a:dst_base + a + S]]))
+        g.remote_dma_fused(tr, local_sem=T.sem["loc"])
+
+    local_each = sum(len(e) for e in plan.values())
+    fa = {h: ("fa%d" % h, sum(arrive.values())) for h in range(4)}
+    ba = {(h, d): ("ba%d_%d" % (h, d), arrive[cores[(rank + 1 + d) % N]]) for h in range(4) for d in range(3)}
+
+    def load(k, name, out, in_):
+        q[k].dma_start(out, in_).then_inc(T.sem[name], 16)
+
+    def ld_b(k, l):
+        load(k, "ldb%d" % l, T.bsb[:, l * M:(l + 1) * M], T.b[:, l * M:(l + 1) * M])
+
+    def ld_e(k, l):
+        a = 192 * (l - 1)
+        load(k, "lde%d" % l, T.ents[:, a:a + 192], T.ent[:, a:a + 192])
+
+    def ld_v(k, l):
+        a = K * (l - 1)
+        load(k, "ldv%d" % l, T.vsb[0:8, a:a + K], T.val[:, a:a + K])
+
+    load("y", "ldsl", T.slr[:, :], T.sl[:, :])
+    ld_b("y", 0)
+    ld_e("y", 1)
+    ld_v("s", 1)
+    ld_b("s", 1)
+
+    v = g.vector
+    k_neg = done("v", v.memset(T.negb[:, :], -1.0))
+    k_oneb = done("v", v.memset(T.oneb[:, :], 1.0))
+    k_onef = done("v", v.memset(T.onef[:, :], 1.0))
+    k_wz = done("v", v.memset(T.w[:, 2304:3840], 0.0))
+    wait("g", k_neg)
+    x = done("g", g.affine_select(T.sel0[0:8, :], T.negb[0:8, :], [[1, 128]], AluOpType.is_ge, 0.0, 0, -16))
+    wait("g", x)
+    k_sel = done("g", g.affine_select(T.sel[0:8, :], T.sel0[0:8, :], [[-1, 128]], AluOpType.is_ge, 0.0, 15, 16))
+    wait("g", k_oneb)
+    k_idb = done("g", g.affine_select(T.idb[:, :], T.oneb[:, :], [[-1, 128]], AluOpType.is_equal, 0.0, 0, 1))
+    wait("g", k_onef)
+    k_idf = done("g", g.affine_select(T.idf[:, :], T.onef[:, :], [[-1, 128]], AluOpType.is_equal, 0.0, 0, 1))
+    wait("s", k_wz)
+    k_wz2 = done("s", g.scalar.activation(T.w[:, 768:2304], T.w[:, 2304:3840], COPY))
+
+    wait("v", ("ldsl", 16))
+    k_sla = done("v", v.tensor_copy(T.sla[:, 0:36], T.slr[:, :]))
+
+    def sl_cols(h, d, n):
+        c = h * 9 + d * 3
+        return T.sla[:, c:c + n] if c % 2 == 0 else T.slb[:, c + 1:c + 1 + n]
+
+    wait("v", ("ldb0", 16), k_sla)
+    k_sh = done("v", v.tensor_copy(T.sh[:, 0:SH], T.bsb[:, 0:M].indirect(sl_cols(0, 0, 9))))
+    wait("g", k_sh)
+    send(0, T.sh, T.w, R, True)
+
+    wait("s", ("ldb0", 16))
+    k_y = {0: done("s", g.scalar.activation(T.w[:, 0:M], T.bsb[:, 0:M], COPY))}
+
+    k_off, k_offb = {}, {}
+
+    def lists(l):
+        a = 192 * (l - 1)
+        wait("v", ("lde%d" % l, 16))
+        x = done("v", v.tensor_scalar(T.entp[:, a:a + 192], T.ents[:, a:a + 192], 2, None, AluOpType.arith_shift_right))
+        k_offb[l] = done("v", v.tensor_copy(T.offb[:, a:a + 192], T.ents[:, a:a + 192]))
+        wait("v", x)
+        k_off[l] = done("v", v.tensor_copy(T.offf[:, a:a + 192], T.entp[:, a:a + 192]))
+
+    lists(1)
+    k_slb = done("v", v.tensor_copy(T.slb[:, 1:37], T.slr[:, :]))
+    k_bz = [done("v", v.memset(T.bk[:, 0:3072], 0.0))]
+
+    k_stg, k_fac, k_acc, k_cst, k_cfac = {}, {}, {}, {}, {}
+    k_a2, k_a3 = {}, {}
+
+    def prep_stage(l):
+        wait("t", k_sel, ("ldv%d" % l, 16))
+        for k in range(3):
+            a = K * (l - 1) + 512 * k
+            if l > 1:
+                wait("t", k_cst[l - 1, k])
+            k_stg[l, k] = done("t", g.tensor.matmul(T.stg[:, 512 * k:512 * k + 512], T.sel[0:8, :], T.vsb[0:8, a:a + 512], True, True))
+
+    def prep_fac(l):
+        if l > 1:
+            wait("t", k_a2[l - 1])
+        for k in range(3):
+            a = K * (l - 1) + 2 * M + 512 * k
+            k_fac[l, k] = done("t", g.tensor.matmul(T.fac[:, 512 * k:512 * k + 512], T.sel[0:8, :], T.vsb[0:8, a:a + 512], True, True))
+
+    def prep_acc(l):
+        wait("t", k_idb, ("ldb%d" % l, 16))
+        if l > 1:
+            wait("t", k_a3[l - 1])
+        for a, e in ((0, 512), (512, M)):
+            done("t", g.tensor.matmul(T.acc[:, a:e], T.idb[:, :], T.bsb[:, l * M + a:l * M + e], True, False))
+
+    def copy_stage(l):
+        for k in range(3):
+            a = K * (l - 1) + 512 * k
+            wait("s", k_stg[l, k])
+            k_cst[l, k] = done("s", g.scalar.activation(T.valf[:, a:a + 512], T.stg[:, 512 * k:512 * k + 512], COPY))
+
+    def copy_fac(l):
+        for k in range(3):
+            a = K * (l - 1) + 2 * M + 512 * k
+            wait("s", k_fac[l, k])
+            k_cfac[l] = done("s", g.scalar.activation(T.valf[:, a:a + 512], T.fac[:, 512 * k:512 * k + 512], COPY))
+
+    prep_stage(1)
+    prep_fac(1)
+    prep_acc(1)
+    copy_stage(1)
+    copy_fac(1)
+
+    s_zero = {1: (RS, RS + 2304), 2: (3072, 5376), 3: (5376, 7680)}
+    v_zero = {1: (7680, 9216), 2: (9216, 10752), 3: (10752, 12288)}
+
+    for l in range(1, 5):
+        win = T.w[:, 0:R + SH * l]
+        off = [T.offf[:, 192 * (l - 1) + 48 * e:192 * (l - 1) + 48 * e + 48] for e in range(4)]
+        base = K * (l - 1)
+        k_raw = []
+        wait("s", fa[l - 1], k_off[l], k_wz, k_wz2, k_y[l - 1])
+        if l > 1:
+            wait("s", k_a3[l - 1])
+        for e in (2, 3):
+            k_raw.append(done("s", g.scalar.activation(T.raw[:, (e - 2) * M:(e - 1) * M], win.indirect(off[e]), COPY)))
+        wait("v", fa[l - 1], k_off[l], k_wz, k_wz2, k_y[l - 1], k_cst[l, 1])
+        k_p0 = done("v", v.tensor_tensor(T.p0[:, :], win.indirect(off[0]), T.valf[:, base:base + M], MUL))
+        wait("v", k_cst[l, 2])
+        k_p1 = done("v", v.tensor_tensor(T.p1[:, :], win.indirect(off[1]), T.valf[:, base + M:base + 2 * M], MUL))
+        wait("t", k_p0, k_idf)
+        for a, e in ((0, 512), (512, M)):
+            k_acc[l] = done("t", g.tensor.matmul(T.acc[:, a:e], T.idf[:, :], T.p0[:, a:e], False, True))
+        if l < 4:
+            wait("y", fa[l - 1])
+            ld_v("y", l + 1)
+            ld_e("y", l + 1)
+            ld_b("y", l + 1)
+            prep_stage(l + 1)
+            copy_stage(l + 1)
+            a, e = s_zero[l]
+            wait("s", k_bz[0])
+            k_bz.append(done("s", g.scalar.activation(T.bk[:, a:e], T.bk[:, 0:e - a], COPY)))
+        wait("v", k_raw[0], k_raw[1], k_fac[l, 2], k_cfac[l])
+        k_m = done("v", v.tensor_tensor(T.fac[:, :], T.raw[:, :], T.fac[:, :], MUL))
+        wait("v", k_p1, k_m)
+        x = done("v", v.tensor_tensor(T.t1[:, :], T.fac[:, 0:M], T.p1[:, :], ADD))
+        wait("v", x)
+        k_a2[l] = done("v", v.tensor_tensor(T.t2[:, :], T.fac[:, M:2 * M], T.t1[:, :], ADD))
+        wait("v", k_a2[l], k_acc[l])
+        k_a3[l] = k_y[l] = done("v", v.tensor_tensor(T.w[:, l * M:(l + 1) * M], T.acc[:, 0:M], T.t2[:, :], ADD))
+        if l < 4:
+            wait("v", k_a3[l], k_sla, k_slb)
+            k_sh = done("v", v.tensor_copy(T.sh[:, l * SH:(l + 1) * SH], T.w[:, 0:R].indirect(sl_cols(l, 0, 9))))
+            wait("g", k_sh)
+            send(l, T.sh, T.w, R, True)
+            prep_fac(l + 1)
+            prep_acc(l + 1)
+            copy_fac(l + 1)
+            lists(l + 1)
+            a, e = v_zero[l]
+            k_bz.append(done("v", v.memset(T.bk[:, a:e], 0.0)))
+
+    k_z = k_a3[4]
+    stores = 0
+    k_o = k_a3[4]
+    for l in range(4, -1, -1):
+        if l < 4:
+            a = RS + 4 * SH * l
+            x = done("v", v.tensor_tensor(T.u1[:, :], T.bk[:, a:a + 4 * SH:2], T.bk[:, a + 1:a + 4 * SH:2], ADD))
+            wait("v", x)
+            k_rs = done("v", v.tensor_tensor(T.rsum[:, l * SH:(l + 1) * SH], T.u1[:, 0:2 * SH:2], T.u1[:, 1:2 * SH:2], ADD))
+            wait("g", k_rs)
+            send(l, T.rsum, T.rc, 0, False)
+            wait("v", k_yc)
+            for s in range(4):
+                slot = T.bk[:, K * l + s:K * (l + 1):4]
+                out = T.acc[:, 0:M] if s < 3 else T.w[:, l * M:(l + 1) * M]
+                k_o = done("v", v.tensor_tensor(out, T.acc[:, 0:M], slot, ADD))
+                wait("v", k_o)
+            ds = sorted(range(3), key=lambda d: topo.chip(cores[(rank + 1 + d) % N]) != topo.chip(core))
+            win = T.w[:, 0:M * (l + 1)]
+            for d in ds:
+                a = (l * 3 + d) * S
+                wait("v", ba[l, d])
+                x = done("v", v.tensor_tensor(T.tmp[:, :], win.indirect(sl_cols(l, d, 3)), T.rc[:, a:a + S], ADD))
+                wait("v", x)
+                k_z = done("v", v.tensor_copy(win.indirect(sl_cols(l, d, 3)), T.tmp[:, :]))
+                wait("v", k_z)
+        wait("y", k_z)
+        g.sync.dma_start(T.z[:, l * M:(l + 1) * M], T.w[:, l * M:(l + 1) * M]).then_inc(T.sem["st"], 16)
+        stores += 16
+        if l > 0:
+            wait("s", k_z, k_o)
+            k_yc = done("s", g.scalar.activation(T.acc[:, 0:M], T.w[:, (l - 1) * M:l * M], COPY))
+            bwin = T.bk[:, 0:RS + 4 * SH * l]
+            wait("v", k_z, k_offb[l], *k_bz)
+            for e in range(4):
+                c = 192 * (l - 1) + 48 * e
+                a = K * (l - 1) + M * e
+                k_sc = done("v", v.tensor_tensor(bwin.indirect(T.offb[:, c:c + 48]), T.w[:, l * M:(l + 1) * M], T.valf[:, a:a + M], MUL))
+                wait("v", k_sc)
+    g.sync.wait_ge(T.sem["st"], stores)
+    g.wait_ge(T.sem["loc"], 8 * local_each)
+    wait("v", ("ss", count["ss"]), ("ts", count["ts"]), ("gs", count["gs"]))

@@ -5,6 +5,10 @@ LV, M, S, N = 5, 768, 48, 4
 R, SH = LV * M, (N - 1) * S
 K = 4 * M
 RS = 4 * R
+NV = 1024
+CH = ((1024, 1792), (1792, 2560), (2560, 3072))
+TC = 176
+VC = M - TC
 
 SCRATCH = {
     "w": ("sbuf", [128, R + 4 * SH], "float32"),
@@ -17,13 +21,16 @@ SCRATCH = {
     "offf": ("sbuf", [128, 768], "uint16"),
     "offb": ("sbuf", [128, 768], "uint16"),
     "slr": ("sbuf", [128, 36], "int32"),
+    "slq": ("sbuf", [128, 36], "int32"),
     "sla": ("sbuf", [128, 40], "uint16"),
     "slb": ("sbuf", [128, 40], "uint16"),
-    "p0": ("sbuf", [128, M], "float32"),
-    "p1": ("sbuf", [128, M], "float32"),
-    "raw": ("sbuf", [128, 2 * M], "float32"),
-    "t1": ("sbuf", [128, M], "float32"),
-    "t2": ("sbuf", [128, M], "float32"),
+    "prod": ("sbuf", [128, K], "float32"),
+    "raw": ("sbuf", [128, K - NV], "float32"),
+    "zrep": ("sbuf", [128, 2 * M], "float32"),
+    "bsh": ("sbuf", [128, 4 * SH], "float32"),
+    "c0": ("sbuf", [128, SH], "float32"),
+    "c1": ("sbuf", [128, SH], "float32"),
+    "c2": ("sbuf", [128, SH], "float32"),
     "sh": ("sbuf", [128, 4 * SH], "float32"),
     "rsum": ("sbuf", [128, 4 * SH], "float32"),
     "rc": ("sbuf", [128, 4 * SH], "float32"),
@@ -37,8 +44,8 @@ SCRATCH = {
     "onef": ("sbuf", [128, 128], "float32"),
     "idf": ("sbuf", [128, 128], "float32"),
     "acc": ("psum", [128, 1024], "float32"),
-    "fac": ("psum", [128, 1536], "float32"),
-    "stg": ("psum", [128, 1536], "float32"),
+    "fac": ("psum", [128, 2048], "float32"),
+    "stg": ("psum", [128, 1024], "float32"),
 }
 SEMAPHORES = (["vs", "ss", "ts", "gs", "loc", "st", "ldsl"]
               + ["ldb%d" % l for l in range(5)] + ["lde%d" % l for l in range(1, 5)]
@@ -87,6 +94,9 @@ def rank_program(g, core, T, topo):
         ins.then_inc(T.sem[name], 1)
         count[name] += 1
         return (name, count[name])
+
+    def copy(out, in_):
+        return done("s", g.scalar.activation(out, in_, COPY))
 
     others = [c for c in cores if c != core]
     plan = engine_plan(core, others, topo)
@@ -142,22 +152,30 @@ def rank_program(g, core, T, topo):
     wait("g", k_onef)
     k_idf = done("g", g.affine_select(T.idf[:, :], T.onef[:, :], [[-1, 128]], AluOpType.is_equal, 0.0, 0, 1))
     wait("s", k_wz)
-    k_wz2 = done("s", g.scalar.activation(T.w[:, 768:2304], T.w[:, 2304:3840], COPY))
+    k_wz2 = copy(T.w[:, 768:2304], T.w[:, 2304:3840])
 
     wait("v", ("ldsl", 16))
-    k_sla = done("v", v.tensor_copy(T.sla[:, 0:36], T.slr[:, :]))
+    k_sl = done("v", v.tensor_copy(T.sla[:, 0:9], T.slr[:, 0:9]))
 
     def sl_cols(h, d, n):
         c = h * 9 + d * 3
         return T.sla[:, c:c + n] if c % 2 == 0 else T.slb[:, c + 1:c + 1 + n]
 
-    wait("v", ("ldb0", 16), k_sla)
+    wait("v", ("ldb0", 16), k_sl)
     k_sh = done("v", v.tensor_copy(T.sh[:, 0:SH], T.bsb[:, 0:M].indirect(sl_cols(0, 0, 9))))
     wait("g", k_sh)
     send(0, T.sh, T.w, R, True)
 
+    k_bz = []
+
+    def g_zero(h):
+        a = 3072 + 2304 * h
+        k_bz.append(done("g", g.iota(T.bk[:, a:a + 2304], [[0, 2304]], 0, 0, allow_small_or_imprecise_dtypes=True)))
+
+    g_zero(0)
+
     wait("s", ("ldb0", 16))
-    k_y = {0: done("s", g.scalar.activation(T.w[:, 0:M], T.bsb[:, 0:M], COPY))}
+    k_y = {0: copy(T.w[:, 0:M], T.bsb[:, 0:M])}
 
     k_off, k_offb = {}, {}
 
@@ -165,110 +183,130 @@ def rank_program(g, core, T, topo):
         a = 192 * (l - 1)
         wait("v", ("lde%d" % l, 16))
         x = done("v", v.tensor_scalar(T.entp[:, a:a + 192], T.ents[:, a:a + 192], 2, None, AluOpType.arith_shift_right))
-        k_offb[l] = done("v", v.tensor_copy(T.offb[:, a:a + 192], T.ents[:, a:a + 192]))
         wait("v", x)
         k_off[l] = done("v", v.tensor_copy(T.offf[:, a:a + 192], T.entp[:, a:a + 192]))
 
-    lists(1)
-    k_slb = done("v", v.tensor_copy(T.slb[:, 1:37], T.slr[:, :]))
-    k_bz = [done("v", v.memset(T.bk[:, 0:3072], 0.0))]
+    def slots(l):
+        a = 192 * (l - 1)
+        k_offb[l] = done("v", v.tensor_copy(T.offb[:, a:a + 192], T.ents[:, a:a + 192]))
 
-    k_stg, k_fac, k_acc, k_cst, k_cfac = {}, {}, {}, {}, {}
-    k_a2, k_a3 = {}, {}
+    lists(1)
+    for h in range(1, 4):
+        x = done("v", v.tensor_scalar(T.slq[:, 9 * h:9 * h + 9], T.slr[:, 9 * h:9 * h + 9], -M * h, None, ADD))
+    done("v", v.tensor_copy(T.slb[:, 1:10], T.slr[:, 0:9]))
+    wait("v", x)
+    done("v", v.tensor_copy(T.sla[:, 9:36], T.slq[:, 9:36]))
+    k_sl = done("v", v.tensor_copy(T.slb[:, 10:37], T.slq[:, 9:36]))
+    k_bz0 = done("v", v.memset(T.bk[:, 0:3072], 0.0))
+    k_bz.append(k_bz0)
+
+    k_fac, k_acc, k_cst, k_cfac, k_m, k_a3 = {}, {}, {}, {}, {}, {}
+    halves = ((0, 512), (512, M))
+    stage = ((0, 512), (512, NV))
+    quarters = tuple((a, a + 512) for a in range(0, K - NV, 512))
 
     def prep_stage(l):
+        base = K * (l - 1)
         wait("t", k_sel, ("ldv%d" % l, 16))
-        for k in range(3):
-            a = K * (l - 1) + 512 * k
-            if l > 1:
-                wait("t", k_cst[l - 1, k])
-            k_stg[l, k] = done("t", g.tensor.matmul(T.stg[:, 512 * k:512 * k + 512], T.sel[0:8, :], T.vsb[0:8, a:a + 512], True, True))
+        if l > 1:
+            wait("t", k_cst[l - 1])
+        for a, e in stage:
+            k = done("t", g.tensor.matmul(T.stg[:, a:e], T.sel[0:8, :], T.vsb[0:8, base + a:base + e], True, True))
+            wait("s", k)
+            k_cst[l] = copy(T.valf[:, base + a:base + e], T.stg[:, a:e])
 
     def prep_fac(l):
-        if l > 1:
-            wait("t", k_a2[l - 1])
-        for k in range(3):
-            a = K * (l - 1) + 2 * M + 512 * k
-            k_fac[l, k] = done("t", g.tensor.matmul(T.fac[:, 512 * k:512 * k + 512], T.sel[0:8, :], T.vsb[0:8, a:a + 512], True, True))
+        for a, e in quarters:
+            k_fac[l] = done("t", g.tensor.matmul(T.fac[:, a:e], T.sel[0:8, :], T.vsb[0:8, K * (l - 1) + NV + a:K * (l - 1) + NV + e], True, True))
+
+    def copy_fac(l):
+        for a, e in quarters:
+            k_cfac[l] = copy(T.valf[:, K * (l - 1) + NV + a:K * (l - 1) + NV + e], T.fac[:, a:e])
 
     def prep_acc(l):
         wait("t", k_idb, ("ldb%d" % l, 16))
         if l > 1:
             wait("t", k_a3[l - 1])
-        for a, e in ((0, 512), (512, M)):
+        for a, e in halves:
             done("t", g.tensor.matmul(T.acc[:, a:e], T.idb[:, :], T.bsb[:, l * M + a:l * M + e], True, False))
 
-    def copy_stage(l):
-        for k in range(3):
-            a = K * (l - 1) + 512 * k
-            wait("s", k_stg[l, k])
-            k_cst[l, k] = done("s", g.scalar.activation(T.valf[:, a:a + 512], T.stg[:, 512 * k:512 * k + 512], COPY))
-
-    def copy_fac(l):
-        for k in range(3):
-            a = K * (l - 1) + 2 * M + 512 * k
-            wait("s", k_fac[l, k])
-            k_cfac[l] = done("s", g.scalar.activation(T.valf[:, a:a + 512], T.fac[:, 512 * k:512 * k + 512], COPY))
+    def shown_b(l):
+        wait("s", ("ldb%d" % l, 16), k_sl)
+        return copy(T.bsh[:, l * SH:(l + 1) * SH], T.bsb[:, l * M:(l + 1) * M].indirect(sl_cols(l, 0, 9)))
 
     prep_stage(1)
     prep_fac(1)
     prep_acc(1)
-    copy_stage(1)
-    copy_fac(1)
-
-    s_zero = {1: (RS, RS + 2304), 2: (3072, 5376), 3: (5376, 7680)}
-    v_zero = {1: (7680, 9216), 2: (9216, 10752), 3: (10752, 12288)}
+    k_bsh = shown_b(1)
 
     for l in range(1, 5):
         win = T.w[:, 0:R + SH * l]
-        off = [T.offf[:, 192 * (l - 1) + 48 * e:192 * (l - 1) + 48 * e + 48] for e in range(4)]
-        base = K * (l - 1)
+        blk = [T.prod[:, e * M:(e + 1) * M] for e in range(4)]
+        base, col = K * (l - 1), 192 * (l - 1)
         k_raw = []
         wait("s", fa[l - 1], k_off[l], k_wz, k_wz2, k_y[l - 1])
-        if l > 1:
-            wait("s", k_a3[l - 1])
-        for e in (2, 3):
-            k_raw.append(done("s", g.scalar.activation(T.raw[:, (e - 2) * M:(e - 1) * M], win.indirect(off[e]), COPY)))
-        wait("v", fa[l - 1], k_off[l], k_wz, k_wz2, k_y[l - 1], k_cst[l, 1])
-        k_p0 = done("v", v.tensor_tensor(T.p0[:, :], win.indirect(off[0]), T.valf[:, base:base + M], MUL))
-        wait("v", k_cst[l, 2])
-        k_p1 = done("v", v.tensor_tensor(T.p1[:, :], win.indirect(off[1]), T.valf[:, base + M:base + 2 * M], MUL))
-        wait("t", k_p0, k_idf)
-        for a, e in ((0, 512), (512, M)):
-            k_acc[l] = done("t", g.tensor.matmul(T.acc[:, a:e], T.idf[:, :], T.p0[:, a:e], False, True))
+        for a, e in CH:
+            k_raw.append(copy(T.raw[:, a - NV:e - NV], win.indirect(T.offf[:, col + a // 16:col + e // 16])))
+        wait("v", fa[l - 1], k_off[l], k_wz, k_wz2, k_y[l - 1], k_cst[l])
+        k_p = [done("v", v.tensor_tensor(T.prod[:, 0:NV], win.indirect(T.offf[:, col:col + NV // 16]), T.valf[:, base:base + NV], MUL))]
+        wait("t", k_p[0], k_idf)
+        for a, e in halves:
+            k_acc[l] = done("t", g.tensor.matmul(T.acc[:, a:e], T.idf[:, :], T.prod[:, a:e], False, True))
+
+        def product(i):
+            a, e = CH[i]
+            wait("v", k_raw[i], k_fac[l])
+            k_p.append(done("v", v.tensor_tensor(T.prod[:, a:e], T.raw[:, a - NV:e - NV], T.fac[:, a - NV:e - NV], MUL)))
+
+        cs = [T.bsh[:, l * SH:(l + 1) * SH], T.c0[:, :], T.c1[:, :], T.c2[:, :], T.sh[:, l * SH:(l + 1) * SH]] if l < 4 else None
+        k_c = [k_bsh]
+
+        def shown(e):
+            wait("v", k_sl, k_p[e], k_c[-1])
+            k_c.append(done("v", v.tensor_tensor(cs[e + 1], blk[e].indirect(sl_cols(l, 0, 9)), cs[e], ADD)))
+
+        product(0)
+        if l < 4:
+            shown(0)
+        product(1)
+        if l < 4:
+            shown(1)
+        product(2)
+        k_m[l] = k_p[3]
+        if l < 4:
+            shown(2)
+            shown(3)
+            wait("g", k_c[-1])
+            send(l, T.sh, T.w, R, True)
+            g_zero(l)
+        for e in range(1, 4):
+            wait("v", k_acc[l], k_p[e])
+            out = T.acc[:, 0:M] if e < 3 else T.w[:, l * M:(l + 1) * M]
+            k = done("v", v.tensor_tensor(out, T.acc[:, 0:M], blk[e], ADD))
+            wait("v", k)
+        k_a3[l] = k_y[l] = k
         if l < 4:
             wait("y", fa[l - 1])
             ld_v("y", l + 1)
-            ld_e("y", l + 1)
             ld_b("y", l + 1)
+            ld_e("y", l + 1)
             prep_stage(l + 1)
-            copy_stage(l + 1)
-            a, e = s_zero[l]
-            wait("s", k_bz[0])
-            k_bz.append(done("s", g.scalar.activation(T.bk[:, a:e], T.bk[:, 0:e - a], COPY)))
-        wait("v", k_raw[0], k_raw[1], k_fac[l, 2], k_cfac[l])
-        k_m = done("v", v.tensor_tensor(T.fac[:, :], T.raw[:, :], T.fac[:, :], MUL))
-        wait("v", k_p1, k_m)
-        x = done("v", v.tensor_tensor(T.t1[:, :], T.fac[:, 0:M], T.p1[:, :], ADD))
-        wait("v", x)
-        k_a2[l] = done("v", v.tensor_tensor(T.t2[:, :], T.fac[:, M:2 * M], T.t1[:, :], ADD))
-        wait("v", k_a2[l], k_acc[l])
-        k_a3[l] = k_y[l] = done("v", v.tensor_tensor(T.w[:, l * M:(l + 1) * M], T.acc[:, 0:M], T.t2[:, :], ADD))
-        if l < 4:
-            wait("v", k_a3[l], k_sla, k_slb)
-            k_sh = done("v", v.tensor_copy(T.sh[:, l * SH:(l + 1) * SH], T.w[:, 0:R].indirect(sl_cols(l, 0, 9))))
-            wait("g", k_sh)
-            send(l, T.sh, T.w, R, True)
+            wait("t", k_m[l])
             prep_fac(l + 1)
             prep_acc(l + 1)
-            copy_fac(l + 1)
+            if l < 3:
+                k_bsh = shown_b(l + 1)
+            wait("s", k_bz0)
+            a = RS + M * (l - 1)
+            k_bz.append(copy(T.bk[:, a:a + M], T.bk[:, 0:M]))
             lists(l + 1)
-            a, e = v_zero[l]
-            k_bz.append(done("v", v.memset(T.bk[:, a:e], 0.0)))
+        else:
+            wait("s", k_m[4])
+            copy_fac(4)
+    slots(4)
 
     k_z = k_a3[4]
     stores = 0
-    k_o = k_a3[4]
     for l in range(4, -1, -1):
         if l < 4:
             a = RS + 4 * SH * l
@@ -277,14 +315,24 @@ def rank_program(g, core, T, topo):
             k_rs = done("v", v.tensor_tensor(T.rsum[:, l * SH:(l + 1) * SH], T.u1[:, 0:2 * SH:2], T.u1[:, 1:2 * SH:2], ADD))
             wait("g", k_rs)
             send(l, T.rsum, T.rc, 0, False)
+            wait("t", k_sc, k_cst[4])
+            for s in range(4):
+                k_t = done("t", g.tensor.matmul(T.stg[:, 0:TC], T.idf[:, :], T.bk[:, K * l + 4 * VC + s:K * (l + 1):4], s == 0, s == 3))
             wait("v", k_yc)
             for s in range(4):
-                slot = T.bk[:, K * l + s:K * (l + 1):4]
-                out = T.acc[:, 0:M] if s < 3 else T.w[:, l * M:(l + 1) * M]
-                k_o = done("v", v.tensor_tensor(out, T.acc[:, 0:M], slot, ADD))
-                wait("v", k_o)
+                slot = T.bk[:, K * l + s:K * l + 4 * VC:4]
+                out = T.acc[:, 0:VC] if s < 3 else T.w[:, l * M:l * M + VC]
+                x = done("v", v.tensor_tensor(out, T.acc[:, 0:VC], slot, ADD))
+                if s < 3:
+                    wait("v", x)
+            wait("v", k_t)
+            tail = T.w[:, l * M + VC:(l + 1) * M]
+            x = done("v", v.tensor_tensor(tail, T.stg[:, 0:TC], tail, ADD))
+            if l > 0:
+                slots(l)
+            wait("v", x)
             ds = sorted(range(3), key=lambda d: topo.chip(cores[(rank + 1 + d) % N]) != topo.chip(core))
-            win = T.w[:, 0:M * (l + 1)]
+            win = T.w[:, M * l:M * (l + 1)]
             for d in ds:
                 a = (l * 3 + d) * S
                 wait("v", ba[l, d])
@@ -292,19 +340,27 @@ def rank_program(g, core, T, topo):
                 wait("v", x)
                 k_z = done("v", v.tensor_copy(win.indirect(sl_cols(l, d, 3)), T.tmp[:, :]))
                 wait("v", k_z)
+        zl = T.w[:, l * M:(l + 1) * M]
         wait("y", k_z)
-        g.sync.dma_start(T.z[:, l * M:(l + 1) * M], T.w[:, l * M:(l + 1) * M]).then_inc(T.sem["st"], 16)
+        g.sync.dma_start(T.z[:, l * M:(l + 1) * M], zl).then_inc(T.sem["st"], 16)
         stores += 16
         if l > 0:
-            wait("s", k_z, k_o)
-            k_yc = done("s", g.scalar.activation(T.acc[:, 0:M], T.w[:, (l - 1) * M:l * M], COPY))
+            wait("s", k_z)
+            copy(T.zrep[:, 0:M], zl)
+            k_rep = copy(T.zrep[:, M:2 * M], zl)
+            k_yc = copy(T.acc[:, 0:VC], T.w[:, (l - 1) * M:(l - 1) * M + VC])
+            base, col = K * (l - 1), 192 * (l - 1)
             bwin = T.bk[:, 0:RS + 4 * SH * l]
-            wait("v", k_z, k_offb[l], *k_bz)
-            for e in range(4):
-                c = 192 * (l - 1) + 48 * e
-                a = K * (l - 1) + M * e
-                k_sc = done("v", v.tensor_tensor(bwin.indirect(T.offb[:, c:c + 48]), T.w[:, l * M:(l + 1) * M], T.valf[:, a:a + M], MUL))
+            for a, e, src, need in ((0, M, zl, [k_z, k_offb[l], k_cst[4]] + k_bz), (M, 2 * M, zl, [k_cfac[l]]),
+                                    (2 * M, K, T.zrep[:, :], [k_rep])):
+                wait("v", *need)
+                k_sc = done("v", v.tensor_tensor(bwin.indirect(T.offb[:, col + a // 16:col + e // 16]), src, T.valf[:, base + a:base + e], MUL))
                 wait("v", k_sc)
+            if l > 1:
+                wait("t", k_cfac[l])
+                prep_fac(l - 1)
+                wait("s", k_fac[l - 1])
+                copy_fac(l - 1)
     g.sync.wait_ge(T.sem["st"], stores)
     g.wait_ge(T.sem["loc"], 8 * local_each)
     wait("v", ("ss", count["ss"]), ("ts", count["ts"]), ("gs", count["gs"]))

@@ -7,8 +7,10 @@ K = 4 * M
 RS = 4 * R
 NV = 1024
 CH = ((1024, 1792), (1792, 2560), (2560, 3072))
-TC = 176
+PB = 512
+TC = 208
 VC = M - TC
+VZ, GZ = 1536, 2688
 
 SCRATCH = {
     "w": ("sbuf", [128, R + 4 * SH], "float32"),
@@ -17,7 +19,6 @@ SCRATCH = {
     "bsb": ("sbuf", [128, R], "bfloat16"),
     "vsb": ("sbuf", [128, 4 * K], "bfloat16"),
     "ents": ("sbuf", [128, 768], "int32"),
-    "entp": ("sbuf", [128, 768], "int32"),
     "offf": ("sbuf", [128, 768], "uint16"),
     "offb": ("sbuf", [128, 768], "uint16"),
     "slr": ("sbuf", [128, 36], "int32"),
@@ -43,9 +44,9 @@ SCRATCH = {
     "idb": ("sbuf", [128, 128], "bfloat16"),
     "onef": ("sbuf", [128, 128], "float32"),
     "idf": ("sbuf", [128, 128], "float32"),
-    "acc": ("psum", [128, 1024], "float32"),
-    "fac": ("psum", [128, 2048], "float32"),
-    "stg": ("psum", [128, 1024], "float32"),
+    "acc": ("psum", [128, 2 * PB], "float32"),
+    "fac": ("psum", [128, 4 * PB], "float32"),
+    "stg": ("psum", [128, 2 * PB], "float32"),
 }
 SEMAPHORES = (["vs", "ss", "ts", "gs", "loc", "st", "ldsl"]
               + ["ldb%d" % l for l in range(5)] + ["lde%d" % l for l in range(1, 5)]
@@ -132,11 +133,12 @@ def rank_program(g, core, T, topo):
         a = K * (l - 1)
         load(k, "ldv%d" % l, T.vsb[0:8, a:a + K], T.val[:, a:a + K])
 
-    load("y", "ldsl", T.slr[:, :], T.sl[:, :])
+    load("s", "ldsl", T.slr[:, :], T.sl[:, :])
     ld_b("y", 0)
+    wait("y", ("ldsl", 16))
+    ld_v("y", 1)
     ld_e("y", 1)
-    ld_v("s", 1)
-    ld_b("s", 1)
+    ld_b("y", 1)
 
     v = g.vector
     k_neg = done("v", v.memset(T.negb[:, :], -1.0))
@@ -169,8 +171,8 @@ def rank_program(g, core, T, topo):
     k_bz = []
 
     def g_zero(h):
-        a = 3072 + 2304 * h
-        k_bz.append(done("g", g.iota(T.bk[:, a:a + 2304], [[0, 2304]], 0, 0, allow_small_or_imprecise_dtypes=True)))
+        a = VZ + GZ * h
+        k_bz.append(done("g", g.iota(T.bk[:, a:a + GZ], [[0, GZ]], 0, 0, allow_small_or_imprecise_dtypes=True)))
 
     g_zero(0)
 
@@ -182,28 +184,26 @@ def rank_program(g, core, T, topo):
     def lists(l):
         a = 192 * (l - 1)
         wait("v", ("lde%d" % l, 16))
-        x = done("v", v.tensor_scalar(T.entp[:, a:a + 192], T.ents[:, a:a + 192], 2, None, AluOpType.arith_shift_right))
-        wait("v", x)
-        k_off[l] = done("v", v.tensor_copy(T.offf[:, a:a + 192], T.entp[:, a:a + 192]))
+        k_off[l] = done("v", v.tensor_scalar(T.offf[:, a:a + 192], T.ents[:, a:a + 192], 0.25, -0.375, MUL, ADD))
 
     def slots(l):
         a = 192 * (l - 1)
         k_offb[l] = done("v", v.tensor_copy(T.offb[:, a:a + 192], T.ents[:, a:a + 192]))
 
-    lists(1)
     for h in range(1, 4):
         x = done("v", v.tensor_scalar(T.slq[:, 9 * h:9 * h + 9], T.slr[:, 9 * h:9 * h + 9], -M * h, None, ADD))
     done("v", v.tensor_copy(T.slb[:, 1:10], T.slr[:, 0:9]))
     wait("v", x)
     done("v", v.tensor_copy(T.sla[:, 9:36], T.slq[:, 9:36]))
     k_sl = done("v", v.tensor_copy(T.slb[:, 10:37], T.slq[:, 9:36]))
-    k_bz0 = done("v", v.memset(T.bk[:, 0:3072], 0.0))
+    k_bz0 = done("v", v.memset(T.bk[:, 0:VZ], 0.0))
     k_bz.append(k_bz0)
+    lists(1)
 
-    k_fac, k_acc, k_cst, k_cfac, k_m, k_a3 = {}, {}, {}, {}, {}, {}
-    halves = ((0, 512), (512, M))
-    stage = ((0, 512), (512, NV))
-    quarters = tuple((a, a + 512) for a in range(0, K - NV, 512))
+    k_fac, k_cst, k_cfac, k_m, k_a3 = {}, {}, {}, {}, {}
+    banks = ((0, PB), (PB, M))
+    stage = ((0, PB), (PB, NV))
+    quarters = tuple((a, a + PB) for a in range(0, K - NV, PB))
 
     def prep_stage(l):
         base = K * (l - 1)
@@ -227,7 +227,7 @@ def rank_program(g, core, T, topo):
         wait("t", k_idb, ("ldb%d" % l, 16))
         if l > 1:
             wait("t", k_a3[l - 1])
-        for a, e in halves:
+        for a, e in banks:
             done("t", g.tensor.matmul(T.acc[:, a:e], T.idb[:, :], T.bsb[:, l * M + a:l * M + e], True, False))
 
     def shown_b(l):
@@ -247,11 +247,12 @@ def rank_program(g, core, T, topo):
         wait("s", fa[l - 1], k_off[l], k_wz, k_wz2, k_y[l - 1])
         for a, e in CH:
             k_raw.append(copy(T.raw[:, a - NV:e - NV], win.indirect(T.offf[:, col + a // 16:col + e // 16])))
-        wait("v", fa[l - 1], k_off[l], k_wz, k_wz2, k_y[l - 1], k_cst[l])
-        k_p = [done("v", v.tensor_tensor(T.prod[:, 0:NV], win.indirect(T.offf[:, col:col + NV // 16]), T.valf[:, base:base + NV], MUL))]
-        wait("t", k_p[0], k_idf)
-        for a, e in halves:
-            k_acc[l] = done("t", g.tensor.matmul(T.acc[:, a:e], T.idf[:, :], T.prod[:, a:e], False, True))
+        wait("v", fa[l - 1], k_off[l], k_wz, k_wz2, k_cst[l], k_y[l - 1])
+        if l < 4:
+            k_p = [done("v", v.tensor_tensor(T.prod[:, 0:NV], win.indirect(T.offf[:, col:col + NV // 16]), T.valf[:, base:base + NV], MUL))]
+        else:
+            k_p = [done("v", v.tensor_tensor(blk[0], win.indirect(T.offf[:, col:col + M // 16]), T.valf[:, base:base + M], MUL))]
+            done("v", v.tensor_tensor(T.prod[:, M:NV], win.indirect(T.offf[:, col + M // 16:col + NV // 16]), T.valf[:, base + M:base + NV], MUL))
 
         def product(i):
             a, e = CH[i]
@@ -279,26 +280,41 @@ def rank_program(g, core, T, topo):
             wait("g", k_c[-1])
             send(l, T.sh, T.w, R, True)
             g_zero(l)
-        for e in range(1, 4):
-            wait("v", k_acc[l], k_p[e])
-            out = T.acc[:, 0:M] if e < 3 else T.w[:, l * M:(l + 1) * M]
-            k = done("v", v.tensor_tensor(out, T.acc[:, 0:M], blk[e], ADD))
-            wait("v", k)
-        k_a3[l] = k_y[l] = k
+
+        def tensor_add(a, e, i, last):
+            wait("t", k_p[i], k_idf)
+            return done("t", g.tensor.matmul(T.acc[:, a:e], T.idf[:, :], T.prod[:, i * M + a:i * M + e], False, last))
+
+        k_acc0 = tensor_add(0, PB, 0, True)
+        tensor_add(PB, M, 0, False)
+        k_acc1 = tensor_add(PB, M, 1, True)
         if l < 4:
             wait("y", fa[l - 1])
             ld_v("y", l + 1)
             ld_b("y", l + 1)
             ld_e("y", l + 1)
-            prep_stage(l + 1)
-            wait("t", k_m[l])
-            prep_fac(l + 1)
-            prep_acc(l + 1)
-            if l < 3:
-                k_bsh = shown_b(l + 1)
             wait("s", k_bz0)
             a = RS + M * (l - 1)
             k_bz.append(copy(T.bk[:, a:a + M], T.bk[:, 0:M]))
+            prep_stage(l + 1)
+            if l < 3:
+                k_bsh = shown_b(l + 1)
+
+        def vector_add(a, e, i, *need):
+            wait("v", k_p[i], *need)
+            out = T.acc[:, a:e] if i < 3 else T.w[:, l * M + a:l * M + e]
+            return done("v", v.tensor_tensor(out, T.acc[:, a:e], T.prod[:, i * M + a:i * M + e], ADD))
+
+        k_h = [k_acc0, k_acc0]
+        for i in range(1, 4):
+            for h in range(2):
+                k_h[h] = vector_add(h * PB // 2, (h + 1) * PB // 2, i, k_h[h])
+        k_acc1 = vector_add(PB, M, 2, k_acc1)
+        k_a3[l] = k_y[l] = vector_add(PB, M, 3, k_acc1)
+        if l < 4:
+            wait("t", k_m[l])
+            prep_fac(l + 1)
+            prep_acc(l + 1)
             lists(l + 1)
         else:
             wait("s", k_m[4])
@@ -318,18 +334,17 @@ def rank_program(g, core, T, topo):
             wait("t", k_sc, k_cst[4])
             for s in range(4):
                 k_t = done("t", g.tensor.matmul(T.stg[:, 0:TC], T.idf[:, :], T.bk[:, K * l + 4 * VC + s:K * (l + 1):4], s == 0, s == 3))
-            wait("v", k_yc)
+            k_h = [k_yc, k_yc]
             for s in range(4):
-                slot = T.bk[:, K * l + s:K * l + 4 * VC:4]
-                out = T.acc[:, 0:VC] if s < 3 else T.w[:, l * M:l * M + VC]
-                x = done("v", v.tensor_tensor(out, T.acc[:, 0:VC], slot, ADD))
-                if s < 3:
-                    wait("v", x)
+                for h, (a, e) in enumerate(((0, VC // 2), (VC // 2, VC))):
+                    wait("v", k_h[h])
+                    out = T.acc[:, a:e] if s < 3 else T.w[:, l * M + a:l * M + e]
+                    k_h[h] = done("v", v.tensor_tensor(out, T.acc[:, a:e], T.bk[:, K * l + 4 * a + s:K * l + 4 * e:4], ADD))
+            if l > 0:
+                slots(l)
             wait("v", k_t)
             tail = T.w[:, l * M + VC:(l + 1) * M]
             x = done("v", v.tensor_tensor(tail, T.stg[:, 0:TC], tail, ADD))
-            if l > 0:
-                slots(l)
             wait("v", x)
             ds = sorted(range(3), key=lambda d: topo.chip(cores[(rank + 1 + d) % N]) != topo.chip(core))
             win = T.w[:, M * l:M * (l + 1)]

from concourse.bass import DstId, RemoteDMATransfer
from concourse.mybir import AluOpType, ActivationFunctionType

LV, M, S, N = 5, 768, 48, 4
R, SH = LV * M, (N - 1) * S
K = 4 * M
RS = 4 * R
NV = 1024
CH = ((1024, 1792), (1792, 2560), (2560, 3072))
PB = 512
TC = 208
VC = M - TC
VZ, GZ = 1536, 2688

SCRATCH = {
    "w": ("sbuf", [128, R + 4 * SH], "float32"),
    "bk": ("sbuf", [128, 4 * (R + 4 * SH)], "float32"),
    "valf": ("sbuf", [128, 4 * K], "float32"),
    "bsb": ("sbuf", [128, R], "bfloat16"),
    "vsb": ("sbuf", [128, 4 * K], "bfloat16"),
    "ents": ("sbuf", [128, 768], "int32"),
    "offf": ("sbuf", [128, 768], "uint16"),
    "offb": ("sbuf", [128, 768], "uint16"),
    "slr": ("sbuf", [128, 36], "int32"),
    "slq": ("sbuf", [128, 36], "int32"),
    "sla": ("sbuf", [128, 40], "uint16"),
    "slb": ("sbuf", [128, 40], "uint16"),
    "prod": ("sbuf", [128, K], "float32"),
    "raw": ("sbuf", [128, K - NV], "float32"),
    "zrep": ("sbuf", [128, 2 * M], "float32"),
    "bsh": ("sbuf", [128, 4 * SH], "float32"),
    "c0": ("sbuf", [128, SH], "float32"),
    "c1": ("sbuf", [128, SH], "float32"),
    "c2": ("sbuf", [128, SH], "float32"),
    "sh": ("sbuf", [128, 4 * SH], "float32"),
    "rsum": ("sbuf", [128, 4 * SH], "float32"),
    "rc": ("sbuf", [128, 4 * SH], "float32"),
    "u1": ("sbuf", [128, 2 * SH], "float32"),
    "tmp": ("sbuf", [128, S], "float32"),
    "negb": ("sbuf", [128, 128], "bfloat16"),
    "sel0": ("sbuf", [128, 128], "bfloat16"),
    "sel": ("sbuf", [128, 128], "bfloat16"),
    "oneb": ("sbuf", [128, 128], "bfloat16"),
    "idb": ("sbuf", [128, 128], "bfloat16"),
    "onef": ("sbuf", [128, 128], "float32"),
    "idf": ("sbuf", [128, 128], "float32"),
    "acc": ("psum", [128, 2 * PB], "float32"),
    "fac": ("psum", [128, 4 * PB], "float32"),
    "stg": ("psum", [128, 2 * PB], "float32"),
}
SEMAPHORES = (["vs", "ss", "ts", "gs", "loc", "st", "ldsl"]
              + ["ldb%d" % l for l in range(5)] + ["lde%d" % l for l in range(1, 5)]
              + ["ldv%d" % l for l in range(1, 5)] + ["fa%d" % h for h in range(4)]
              + ["ba%d_%d" % (h, d) for h in range(4) for d in range(3)])


def engine_plan(src, dsts, topo):
    left = sorted(dsts, key=lambda c: len(topo.engines(src, c)))
    used, plan = set(), {}
    for i, c in enumerate(left):
        free = [e for e in topo.engines(src, c) if e not in used]
        share = sum(1 for x in left[i:] if set(topo.engines(src, x)) == set(topo.engines(src, c)))
        n = 1
        while 2 * n <= len(free) // share and 2 * n <= 4:
            n *= 2
        plan[c] = free[:n]
        used.update(plan[c])
    return plan


def rank_program(g, core, T, topo):
    rank = T.rank_of(core)
    if rank is None:
        return
    ADD, MUL = AluOpType.add, AluOpType.mult
    COPY = ActivationFunctionType.Copy
    cores = list(T.cores)
    q = {"v": g.vector, "s": g.scalar, "t": g.tensor, "g": g, "y": g.sync}
    own = {"v": "vs", "s": "ss", "t": "ts", "g": "gs"}
    count = {"vs": 0, "ss": 0, "ts": 0, "gs": 0}
    seen = {k: {} for k in q}

    def wait(k, *tokens):
        need = {}
        for name, n in tokens:
            if n > need.get(name, 0):
                need[name] = n
        for name, n in need.items():
            if n > seen[k].get(name, 0):
                q[k].wait_ge(T.sem[name], n)
                seen[k][name] = n

    def done(k, ins):
        name = own[k]
        ins.then_inc(T.sem[name], 1)
        count[name] += 1
        return (name, count[name])

    def copy(out, in_):
        return done("s", g.scalar.activation(out, in_, COPY))

    others = [c for c in cores if c != core]
    plan = engine_plan(core, others, topo)
    arrive = {c: len(engine_plan(c, [x for x in cores if x != c], topo)[core]) for c in others}

    def send(h, src, dst, dst_base, forward):
        tr = []
        for d in range(3):
            c = cores[(rank + 1 + d) % N] if forward else cores[(rank - 1 - d) % N]
            rid, pid = topo.addr(c)[:2]
            a = (h * 3 + d) * S
            m = sum(1 << e for e in plan[c])
            sem = T.sem["fa%d" % h] if forward else T.sem["ba%d_%d" % (h, d)]
            tr.append(RemoteDMATransfer(dst_ids=[DstId(rid=rid, pnc=pid)], dma_engine_mask=m, remote_sem=sem,
                                        srcs=[src[:, a:a + S]], dsts=[dst[:, dst_base + a:dst_base + a + S]]))
        g.remote_dma_fused(tr, local_sem=T.sem["loc"])

    local_each = sum(len(e) for e in plan.values())
    fa = {h: ("fa%d" % h, sum(arrive.values())) for h in range(4)}
    ba = {(h, d): ("ba%d_%d" % (h, d), arrive[cores[(rank + 1 + d) % N]]) for h in range(4) for d in range(3)}

    def load(k, name, out, in_):
        q[k].dma_start(out, in_).then_inc(T.sem[name], 16)

    def ld_b(k, l):
        load(k, "ldb%d" % l, T.bsb[:, l * M:(l + 1) * M], T.b[:, l * M:(l + 1) * M])

    def ld_e(k, l):
        a = 192 * (l - 1)
        load(k, "lde%d" % l, T.ents[:, a:a + 192], T.ent[:, a:a + 192])

    def ld_v(k, l):
        a = K * (l - 1)
        load(k, "ldv%d" % l, T.vsb[0:8, a:a + K], T.val[:, a:a + K])

    load("s", "ldsl", T.slr[:, :], T.sl[:, :])
    ld_b("y", 0)
    wait("y", ("ldsl", 16))
    ld_v("y", 1)
    ld_e("y", 1)
    ld_b("y", 1)

    v = g.vector
    k_neg = done("v", v.memset(T.negb[:, :], -1.0))
    k_oneb = done("v", v.memset(T.oneb[:, :], 1.0))
    k_onef = done("v", v.memset(T.onef[:, :], 1.0))
    k_wz = done("v", v.memset(T.w[:, 2304:3840], 0.0))
    wait("g", k_neg)
    x = done("g", g.affine_select(T.sel0[0:8, :], T.negb[0:8, :], [[1, 128]], AluOpType.is_ge, 0.0, 0, -16))
    wait("g", x)
    k_sel = done("g", g.affine_select(T.sel[0:8, :], T.sel0[0:8, :], [[-1, 128]], AluOpType.is_ge, 0.0, 15, 16))
    wait("g", k_oneb)
    k_idb = done("g", g.affine_select(T.idb[:, :], T.oneb[:, :], [[-1, 128]], AluOpType.is_equal, 0.0, 0, 1))
    wait("g", k_onef)
    k_idf = done("g", g.affine_select(T.idf[:, :], T.onef[:, :], [[-1, 128]], AluOpType.is_equal, 0.0, 0, 1))
    wait("s", k_wz)
    k_wz2 = copy(T.w[:, 768:2304], T.w[:, 2304:3840])

    wait("v", ("ldsl", 16))
    k_sl = done("v", v.tensor_copy(T.sla[:, 0:9], T.slr[:, 0:9]))

    def sl_cols(h, d, n):
        c = h * 9 + d * 3
        return T.sla[:, c:c + n] if c % 2 == 0 else T.slb[:, c + 1:c + 1 + n]

    wait("v", ("ldb0", 16), k_sl)
    k_sh = done("v", v.tensor_copy(T.sh[:, 0:SH], T.bsb[:, 0:M].indirect(sl_cols(0, 0, 9))))
    wait("g", k_sh)
    send(0, T.sh, T.w, R, True)

    k_bz = []

    def g_zero(h):
        a = VZ + GZ * h
        k_bz.append(done("g", g.iota(T.bk[:, a:a + GZ], [[0, GZ]], 0, 0, allow_small_or_imprecise_dtypes=True)))

    g_zero(0)

    wait("s", ("ldb0", 16))
    k_y = {0: copy(T.w[:, 0:M], T.bsb[:, 0:M])}

    k_off, k_offb = {}, {}

    def lists(l):
        a = 192 * (l - 1)
        wait("v", ("lde%d" % l, 16))
        k_off[l] = done("v", v.tensor_scalar(T.offf[:, a:a + 192], T.ents[:, a:a + 192], 0.25, -0.375, MUL, ADD))

    def slots(l):
        a = 192 * (l - 1)
        k_offb[l] = done("v", v.tensor_copy(T.offb[:, a:a + 192], T.ents[:, a:a + 192]))

    for h in range(1, 4):
        x = done("v", v.tensor_scalar(T.slq[:, 9 * h:9 * h + 9], T.slr[:, 9 * h:9 * h + 9], -M * h, None, ADD))
    done("v", v.tensor_copy(T.slb[:, 1:10], T.slr[:, 0:9]))
    wait("v", x)
    done("v", v.tensor_copy(T.sla[:, 9:36], T.slq[:, 9:36]))
    k_sl = done("v", v.tensor_copy(T.slb[:, 10:37], T.slq[:, 9:36]))
    k_bz0 = done("v", v.memset(T.bk[:, 0:VZ], 0.0))
    k_bz.append(k_bz0)
    lists(1)

    k_fac, k_cst, k_cfac, k_m, k_a3 = {}, {}, {}, {}, {}
    banks = ((0, PB), (PB, M))
    stage = ((0, PB), (PB, NV))
    quarters = tuple((a, a + PB) for a in range(0, K - NV, PB))

    def prep_stage(l):
        base = K * (l - 1)
        wait("t", k_sel, ("ldv%d" % l, 16))
        if l > 1:
            wait("t", k_cst[l - 1])
        for a, e in stage:
            k = done("t", g.tensor.matmul(T.stg[:, a:e], T.sel[0:8, :], T.vsb[0:8, base + a:base + e], True, True))
            wait("s", k)
            k_cst[l] = copy(T.valf[:, base + a:base + e], T.stg[:, a:e])

    def prep_fac(l):
        for a, e in quarters:
            k_fac[l] = done("t", g.tensor.matmul(T.fac[:, a:e], T.sel[0:8, :], T.vsb[0:8, K * (l - 1) + NV + a:K * (l - 1) + NV + e], True, True))

    def copy_fac(l):
        for a, e in quarters:
            k_cfac[l] = copy(T.valf[:, K * (l - 1) + NV + a:K * (l - 1) + NV + e], T.fac[:, a:e])

    def prep_acc(l):
        wait("t", k_idb, ("ldb%d" % l, 16))
        if l > 1:
            wait("t", k_a3[l - 1])
        for a, e in banks:
            done("t", g.tensor.matmul(T.acc[:, a:e], T.idb[:, :], T.bsb[:, l * M + a:l * M + e], True, False))

    def shown_b(l):
        wait("s", ("ldb%d" % l, 16), k_sl)
        return copy(T.bsh[:, l * SH:(l + 1) * SH], T.bsb[:, l * M:(l + 1) * M].indirect(sl_cols(l, 0, 9)))

    prep_stage(1)
    prep_fac(1)
    prep_acc(1)
    k_bsh = shown_b(1)

    for l in range(1, 5):
        win = T.w[:, 0:R + SH * l]
        blk = [T.prod[:, e * M:(e + 1) * M] for e in range(4)]
        base, col = K * (l - 1), 192 * (l - 1)
        k_raw = []
        wait("s", fa[l - 1], k_off[l], k_wz, k_wz2, k_y[l - 1])
        for a, e in CH:
            k_raw.append(copy(T.raw[:, a - NV:e - NV], win.indirect(T.offf[:, col + a // 16:col + e // 16])))
        wait("v", fa[l - 1], k_off[l], k_wz, k_wz2, k_cst[l], k_y[l - 1])
        if l < 4:
            k_p = [done("v", v.tensor_tensor(T.prod[:, 0:NV], win.indirect(T.offf[:, col:col + NV // 16]), T.valf[:, base:base + NV], MUL))]
        else:
            k_p = [done("v", v.tensor_tensor(blk[0], win.indirect(T.offf[:, col:col + M // 16]), T.valf[:, base:base + M], MUL))]
            done("v", v.tensor_tensor(T.prod[:, M:NV], win.indirect(T.offf[:, col + M // 16:col + NV // 16]), T.valf[:, base + M:base + NV], MUL))

        def product(i):
            a, e = CH[i]
            wait("v", k_raw[i], k_fac[l])
            k_p.append(done("v", v.tensor_tensor(T.prod[:, a:e], T.raw[:, a - NV:e - NV], T.fac[:, a - NV:e - NV], MUL)))

        cs = [T.bsh[:, l * SH:(l + 1) * SH], T.c0[:, :], T.c1[:, :], T.c2[:, :], T.sh[:, l * SH:(l + 1) * SH]] if l < 4 else None
        k_c = [k_bsh]

        def shown(e):
            wait("v", k_sl, k_p[e], k_c[-1])
            k_c.append(done("v", v.tensor_tensor(cs[e + 1], blk[e].indirect(sl_cols(l, 0, 9)), cs[e], ADD)))

        product(0)
        if l < 4:
            shown(0)
        product(1)
        if l < 4:
            shown(1)
        product(2)
        k_m[l] = k_p[3]
        if l < 4:
            shown(2)
            shown(3)
            wait("g", k_c[-1])
            send(l, T.sh, T.w, R, True)
            g_zero(l)

        def tensor_add(a, e, i, last):
            wait("t", k_p[i], k_idf)
            return done("t", g.tensor.matmul(T.acc[:, a:e], T.idf[:, :], T.prod[:, i * M + a:i * M + e], False, last))

        k_acc0 = tensor_add(0, PB, 0, True)
        tensor_add(PB, M, 0, False)
        k_acc1 = tensor_add(PB, M, 1, True)
        if l < 4:
            wait("y", fa[l - 1])
            ld_v("y", l + 1)
            ld_b("y", l + 1)
            ld_e("y", l + 1)
            wait("s", k_bz0)
            a = RS + M * (l - 1)
            k_bz.append(copy(T.bk[:, a:a + M], T.bk[:, 0:M]))
            prep_stage(l + 1)
            if l < 3:
                k_bsh = shown_b(l + 1)

        def vector_add(a, e, i, *need):
            wait("v", k_p[i], *need)
            out = T.acc[:, a:e] if i < 3 else T.w[:, l * M + a:l * M + e]
            return done("v", v.tensor_tensor(out, T.acc[:, a:e], T.prod[:, i * M + a:i * M + e], ADD))

        k_h = [k_acc0, k_acc0]
        for i in range(1, 4):
            for h in range(2):
                k_h[h] = vector_add(h * PB // 2, (h + 1) * PB // 2, i, k_h[h])
        k_acc1 = vector_add(PB, M, 2, k_acc1)
        k_a3[l] = k_y[l] = vector_add(PB, M, 3, k_acc1)
        if l < 4:
            wait("t", k_m[l])
            prep_fac(l + 1)
            prep_acc(l + 1)
            lists(l + 1)
        else:
            wait("s", k_m[4])
            copy_fac(4)
    slots(4)

    k_z = k_a3[4]
    stores = 0
    for l in range(4, -1, -1):
        if l < 4:
            a = RS + 4 * SH * l
            x = done("v", v.tensor_tensor(T.u1[:, :], T.bk[:, a:a + 4 * SH:2], T.bk[:, a + 1:a + 4 * SH:2], ADD))
            wait("v", x)
            k_rs = done("v", v.tensor_tensor(T.rsum[:, l * SH:(l + 1) * SH], T.u1[:, 0:2 * SH:2], T.u1[:, 1:2 * SH:2], ADD))
            wait("g", k_rs)
            send(l, T.rsum, T.rc, 0, False)
            wait("t", k_sc, k_cst[4])
            for s in range(4):
                k_t = done("t", g.tensor.matmul(T.stg[:, 0:TC], T.idf[:, :], T.bk[:, K * l + 4 * VC + s:K * (l + 1):4], s == 0, s == 3))
            k_h = [k_yc, k_yc]
            for s in range(4):
                for h, (a, e) in enumerate(((0, VC // 2), (VC // 2, VC))):
                    wait("v", k_h[h])
                    out = T.acc[:, a:e] if s < 3 else T.w[:, l * M + a:l * M + e]
                    k_h[h] = done("v", v.tensor_tensor(out, T.acc[:, a:e], T.bk[:, K * l + 4 * a + s:K * l + 4 * e:4], ADD))
            if l > 0:
                slots(l)
            wait("v", k_t)
            tail = T.w[:, l * M + VC:(l + 1) * M]
            x = done("v", v.tensor_tensor(tail, T.stg[:, 0:TC], tail, ADD))
            wait("v", x)
            ds = sorted(range(3), key=lambda d: topo.chip(cores[(rank + 1 + d) % N]) != topo.chip(core))
            win = T.w[:, M * l:M * (l + 1)]
            for d in ds:
                a = (l * 3 + d) * S
                wait("v", ba[l, d])
                x = done("v", v.tensor_tensor(T.tmp[:, :], win.indirect(sl_cols(l, d, 3)), T.rc[:, a:a + S], ADD))
                wait("v", x)
                k_z = done("v", v.tensor_copy(win.indirect(sl_cols(l, d, 3)), T.tmp[:, :]))
                wait("v", k_z)
        zl = T.w[:, l * M:(l + 1) * M]
        wait("y", k_z)
        g.sync.dma_start(T.z[:, l * M:(l + 1) * M], zl).then_inc(T.sem["st"], 16)
        stores += 16
        if l > 0:
            wait("s", k_z)
            copy(T.zrep[:, 0:M], zl)
            k_rep = copy(T.zrep[:, M:2 * M], zl)
            k_yc = copy(T.acc[:, 0:VC], T.w[:, (l - 1) * M:(l - 1) * M + VC])
            base, col = K * (l - 1), 192 * (l - 1)
            bwin = T.bk[:, 0:RS + 4 * SH * l]
            for a, e, src, need in ((0, M, zl, [k_z, k_offb[l], k_cst[4]] + k_bz), (M, 2 * M, zl, [k_cfac[l]]),
                                    (2 * M, K, T.zrep[:, :], [k_rep])):
                wait("v", *need)
                k_sc = done("v", v.tensor_tensor(bwin.indirect(T.offb[:, col + a // 16:col + e // 16]), src, T.valf[:, base + a:base + e], MUL))
                wait("v", k_sc)
            if l > 1:
                wait("t", k_cfac[l])
                prep_fac(l - 1)
                wait("s", k_fac[l - 1])
                copy_fac(l - 1)
    g.sync.wait_ge(T.sem["st"], stores)
    g.wait_ge(T.sem["loc"], 8 * local_each)
    wait("v", ("ss", count["ss"]), ("ts", count["ts"]), ("gs", count["gs"]))
